import numpy as np
import ml_dtypes


def mxq(x, axis, fmt="e4m3"):
    dtype, down = {"e4m3": (ml_dtypes.float8_e4m3fn, 7), "e5m2": (ml_dtypes.float8_e5m2, 14)}[fmt]
    v = np.moveaxis(np.asarray(x, np.float32).astype(ml_dtypes.bfloat16).astype(np.float64), axis, -1)
    blocks = v.reshape(v.shape[:-1] + (-1, 32))
    amax = np.abs(blocks).max(-1, keepdims=True)
    byte = np.maximum(np.where(amax > 0, np.frexp(amax)[1] - 1 + 127, 0) - down, 1)
    scale = np.exp2(byte - 127.0)
    codes = (blocks / scale).astype(np.float32).astype(dtype).astype(np.float64)
    return np.moveaxis((codes * scale).reshape(v.shape), -1, axis)


WIDE = False


def mx_kscale(k):
    if not WIDE:
        return np.ones(k)
    levels = np.array([10, -10, 5, -5, 0])
    if k % 512:
        return np.exp2(np.random.permutation(np.resize(levels, k // 32))).repeat(32)
    a = np.empty((k // 512, 16))
    for p in range(k // 512):
        a[p, :8] = np.random.permutation(np.resize(levels, 8))
        for g in range(8):
            far = levels[np.abs(levels - a[p, g]) >= 10]
            a[p, g + 8] = far[np.random.randint(len(far))]
    return np.exp2(a.ravel()).repeat(32)


def f64(x):
    return np.asarray(x).astype(np.float64)


def striped(idx):
    return np.tile(np.asarray(idx).reshape(-1, 16).T, (8, 1)).astype(np.uint16)


def unstriped(offs):
    return offs[:16].T.reshape(-1).astype(np.int64)


E2M1 = np.array([0.0, 0.5, 1.0, 1.5, 2.0, 3.0, 4.0, 6.0, -0.0, -0.5, -1.0, -1.5, -2.0, -3.0, -4.0, -6.0])


def pack_weight(w, fmt):
    k, n = w.shape
    w = f64(np.asarray(w, np.float32).astype(ml_dtypes.bfloat16)).reshape(k // 32, 32, n)
    amax = np.abs(w).max(1)
    if fmt == "e4m3":
        byte = np.frexp(amax)[1] - 1 + 127 - 7
    else:
        mant, ex = np.frexp(amax / 6.0)
        byte = np.where(mant > 0.5, ex, ex - 1) + 127
    byte = np.clip(np.where(amax > 0, byte, 1), 1, 254)
    scaled = (w * np.exp2(127.0 - byte)[:, None, :]).reshape(k, n).astype(np.float32)
    by_word = np.ascontiguousarray(scaled.reshape(k // 512, 128, 4, n).transpose(0, 1, 3, 2))
    if fmt == "e4m3":
        words = by_word.astype(ml_dtypes.float8_e4m3fn).view(np.uint8)
    else:
        c = by_word.astype(ml_dtypes.float4_e2m1fn).view(np.uint8) & 0xF
        words = (c[..., 0::2] | (c[..., 1::2] << 4)).reshape(k // 512, 128, 2 * n)
    return np.ascontiguousarray(words), np.ascontiguousarray(byte.astype(np.uint8).reshape(k // 512, 16, n))


def unpack_weight(words, scales, fmt):
    g, _, n = scales.shape
    words = np.ascontiguousarray(words).reshape(g, 128, n, -1)
    if fmt == "e4m3":
        vals = words.view(ml_dtypes.float8_e4m3fn).astype(np.float64)
    else:
        nib = np.empty((g, 128, n, 4), np.uint8)
        nib[..., 0::2] = words & 0xF
        nib[..., 1::2] = words >> 4
        vals = E2M1[nib]
    vals = vals * np.repeat(np.exp2(scales.astype(np.float64) - 127.0), 8, axis=1)[..., None]
    return vals.transpose(0, 1, 3, 2).reshape(g * 512, n)


D, E, T, I, G, U, Q = 512, 512, 4096, 1024, 64, 512, 128


def setup_inputs():
    n = np.random.standard_normal
    idx = np.random.permutation(T)[:I]
    idx2 = np.random.permutation(U)[:G]
    fd = mx_kscale(D)
    fe = mx_kscale(E)
    keysp = pack_weight(n((D, T)) / fd[:, None], "e4m3")
    valsp = pack_weight(n((E, T)) / fe[:, None], "e4m3")
    return {
        "query": (n((D, Q)) * 0.6 / np.sqrt(D) * fd[:, None]).astype(np.float32),
        "keys_words": keysp[0],
        "keys_scales": keysp[1],
        "ptab": (n((Q, U)) * 0.25).astype(np.float32),
        "gout": (n((E, Q)) * 1 / np.sqrt(E) * fe[:, None]).astype(np.float32),
        "vals_words": valsp[0],
        "vals_scales": valsp[1],
        "old": (0.5 * n((Q, U))).astype(np.float32),
        "offs": striped(idx),
        "offs2": striped(idx2),
    }


def reference(query, keys_words, keys_scales, ptab, gout, vals_words, vals_scales, old, offs, offs2):
    idx = unstriped(offs)
    idx2 = unstriped(offs2)
    keysu = unpack_weight(keys_words, keys_scales, "e4m3")
    valsu = unpack_weight(vals_words, vals_scales, "e4m3")
    queryq = mxq(f64(query), 0, "e4m3")
    keysidxg = keysu[:, idx]
    a = queryq.T @ keysidxg
    x1 = np.exp(a)
    goutq = mxq(f64(gout), 0, "e4m3")
    valsidxg = valsu[:, idx]
    c0 = goutq.T @ valsidxg
    s = x1.reshape(Q, G, I // G).sum(axis=2)
    m1 = (x1 * c0).reshape(Q, G, I // G).sum(axis=2) / s
    tp = np.exp(f64(ptab)[:, idx2])
    p = np.exp(np.log(s) * tp)
    z = np.sum(p, axis=1, keepdims=True)
    dz = np.sum(p * m1, axis=1, keepdims=True) / np.square(z) * (-1.0)
    dp = 1.0 / z * m1 + dz
    dtp = dp * p * np.log(s)
    gs = dtp * tp * 8.0
    gf = np.zeros((Q, U))
    gf[:, idx2] = gs
    y = f64(old) + gf
    return y

@@ -1,0 +1,156 @@
+from contextlib import ExitStack
+
+import concourse.mybir as mybir
+
+D, E, T, I, G, U, Q = 512, 512, 4096, 1024, 64, 512, 128
+FLOPS = 2 * Q * I * (D + E)
+
+F32 = mybir.dt.float32
+BF16 = mybir.dt.bfloat16
+I32 = mybir.dt.int32
+U32 = mybir.dt.uint32
+U16 = mybir.dt.uint16
+U8 = mybir.dt.uint8
+FP8X4 = mybir.dt.float8_e4m3fn_x4
+ALU = mybir.AluOpType
+ACT = mybir.ActivationFunctionType
+AXIS = mybir.AxisListType
+
+P = 128
+PACK = 4
+HALF = 512
+HALVES = I // HALF
+PAGE = I // G
+PAGES = HALF // PAGE
+LIST = 16
+VALS_ROW0 = 4
+
+
+def load_scales(queue, plane, scales, row0):
+    for r in range(4):
+        queue.dma_start(out=plane[row0 + r : P : 32, :].bitcast(I32), in_=scales[0, r:16:4, :].bitcast(I32))
+
+
+def tile_attend_bpagepower_kernel(tc, query, keys_words, keys_scales, ptab, gout, vals_words, vals_scales, old, offs, offs2, out):
+    nc = tc.nc
+    with ExitStack() as ctx:
+        sb = ctx.enter_context(tc.tile_pool(name="sb", bufs=1))
+        ps = ctx.enter_context(tc.psum_pool(name="ps", bufs=1))
+
+        slots = sb.tile([P, I // LIST], U16)
+        pages = sb.tile([P, G // LIST], U16)
+        k_plane = sb.tile([P, T], U8, align_bytes=64, tag="k_plane")
+        v_plane = sb.tile([P, T], U8, align_bytes=64)
+        k_store = sb.tile([P, T], U32, align_bytes=64, tag="k_store")
+        v_store = sb.tile([P, T], U32, align_bytes=64, tag="v_store")
+        q_raw = sb.tile([P, PACK, Q], F32)
+        g_raw = sb.tile([P, PACK, Q], F32)
+        ptab_sb = sb.tile([P, U], F32)
+        old_sb = sb.tile([P, U], F32)
+        placed = sb.tile([P, U], F32)
+
+        nc.vector.memset(k_plane[:].bitcast(I32), 0)
+        nc.vector.memset(placed[:], 0.0)
+        nc.vector.memset(v_plane[:].bitcast(I32), 0)
+
+        load_scales(nc.sync, k_plane, keys_scales, 0)
+        nc.sync.dma_start(slots[:], offs)
+        nc.sync.dma_start(pages[:], offs2)
+        nc.sync.dma_start(out=q_raw[:], in_=query.rearrange("(p j) q -> p j q", j=PACK))
+        nc.sync.dma_start(out=k_store[:].bitcast(I32), in_=keys_words[0].rearrange("p n t -> p (n t)").bitcast(I32))
+        load_scales(nc.scalar, v_plane, vals_scales, VALS_ROW0)
+        nc.sync.dma_start(out=g_raw[:], in_=gout.rearrange("(p j) q -> p j q", j=PACK))
+        nc.sync.dma_start(out=ptab_sb[:], in_=ptab)
+        nc.sync.dma_start(out=v_store[:].bitcast(I32), in_=vals_words[0].rearrange("p n t -> p (n t)").bitcast(I32))
+        nc.sync.dma_start(out=old_sb[:], in_=old)
+
+        def quantise(raw, name, tag):
+            grouped = sb.tile([P, Q, PACK], BF16, align_bytes=64, name=name + "_bf16")
+            codes = sb.tile([P, Q], U32, align_bytes=64, name=name + "_codes", tag=tag)
+            scales = sb.tile([P, Q], U8, align_bytes=64, name=name + "_scales")
+            nc.scalar.copy(out=grouped[:], in_=raw[:].rearrange("p j q -> p q j"))
+            nc.vector.quantize_mx(out=codes[:].bitcast(FP8X4), scales=scales[:], in_=grouped[:].rearrange("p q j -> p (q j)"))
+            return codes, scales
+
+        k_scales = sb.tile([P, I], U8, align_bytes=64)
+        v_scales = sb.tile([P, I], U8, align_bytes=64)
+        nc.vector.tensor_copy(k_scales[:], k_plane[:].indirect(slots[:]))
+        q_codes, q_scales = quantise(q_raw, "q", "k_plane")
+
+        nc.vector.tensor_copy(v_scales[:], v_plane[:].indirect(slots[:]))
+
+        def product(store, scales, row0, codes_q, scales_q, h, name):
+            cols = slice(h * HALF, (h + 1) * HALF)
+            words = sb.tile([P, HALF], U32, align_bytes=64, name="%s_words%d" % (name, h))
+            bank = ps.tile([P, HALF], F32, name="%s_bank%d" % (name, h))
+            nc.vector.tensor_copy(words[:], store[:].indirect(slots[:, h * HALF // LIST : (h + 1) * HALF // LIST]))
+            nc.tensor.matmul_mx(
+                out=bank[:],
+                lhsT=codes_q[:].bitcast(FP8X4),
+                lhsT_scale=scales_q[:],
+                rhs=words[:].bitcast(FP8X4),
+                rhs_scale=scales[row0:P, cols],
+                start=True,
+                stop=True,
+            )
+            return bank
+
+        x1 = []
+        for h in range(HALVES):
+            bank = product(k_store, k_scales, 0, q_codes, q_scales, h, "k")
+            x = sb.tile([P, HALF], F32, name="x1_%d" % h)
+            nc.scalar.activation(x[:], bank[:], ACT.Exp)
+            x1.append(x)
+        g_codes, g_scales = quantise(g_raw, "g", "k_store")
+        log_power = sb.tile([P, G], F32)
+        powers = sb.tile([P, 2, G], F32)
+        nc.vector.tensor_copy(log_power[:], ptab_sb[:].indirect(pages[:]))
+        nc.scalar.activation(powers[:, 0, :], log_power[:], ACT.Exp)
+        nc.scalar.activation(powers[:, 1, :], powers[:, 0, :], ACT.Copy, bias=-1.0)
+
+        s = sb.tile([P, G], F32)
+        for h in range(HALVES):
+            nc.vector.tensor_reduce(
+                out=s[:, h * PAGES : (h + 1) * PAGES], in_=x1[h][:].rearrange("p (g i) -> p g i", i=PAGE), axis=AXIS.X, op=ALU.add
+            )
+        log_s = sb.tile([P, G], F32)
+        nc.scalar.activation(log_s[:], s[:], ACT.Ln)
+
+        c_banks = [product(v_store, v_scales, VALS_ROW0, g_codes, g_scales, h, "v") for h in range(HALVES)]
+
+        expo = sb.tile([P, 2, G], F32, align_bytes=64, tag="v_store")
+        neg_top = sb.tile([P, 1], F32)
+        nc.vector.tensor_tensor(expo[:], powers[:], log_s[:].unsqueeze(1).to_broadcast([P, 2, G]), ALU.mult)
+        nc.vector.tensor_reduce(out=neg_top[:], in_=expo[:, 0, :], axis=AXIS.X, op=ALU.max, negate=True)
+
+        part = sb.tile([P, G], F32)
+        part_over_s = sb.tile([P, G], F32)
+        z = sb.tile([P, 1], F32)
+        inv_z = sb.tile([P, 1], F32)
+        share = sb.tile([P, G], F32)
+        factor = sb.tile([P, G], F32)
+        nc.scalar.activation(part[:], expo[:, 0, :], ACT.Exp, bias=neg_top[:], accum_out=z[:])
+        nc.scalar.activation(part_over_s[:], expo[:, 1, :], ACT.Exp, bias=neg_top[:])
+
+        weighted = sb.tile([P, I], F32)
+        nc.vector.tensor_tensor(weighted[:, 0:HALF], c_banks[0][:], x1[0][:], ALU.mult)
+        nc.vector.tensor_tensor(weighted[:, HALF:I], c_banks[1][:], x1[1][:], ALU.mult)
+        nc.vector.reciprocal(inv_z[:], z[:])
+        nc.scalar.activation(share[:], part[:], ACT.Copy, scale=inv_z[:])
+        nc.scalar.activation(factor[:], expo[:, 0, :], ACT.Copy, scale=inv_z[:])
+
+        page_sum = sb.tile([P, G], F32)
+        nc.vector.tensor_reduce(out=page_sum[:], in_=weighted[:].rearrange("p (g i) -> p g i", i=PAGE), axis=AXIS.X, op=ALU.add)
+
+        term = sb.tile([P, G], F32)
+        term_sum = sb.tile([P, 1], F32)
+        centred = sb.tile([P, G], F32)
+        nc.vector.scalar_tensor_tensor(term[:], page_sum[:], -8.0, part_over_s[:], ALU.mult, ALU.mult, accum_out=term_sum[:])
+        nc.vector.scalar_tensor_tensor(centred[:], share[:], term_sum[:], term[:], ALU.mult, ALU.subtract)
+        nc.vector.tensor_tensor(placed[:].indirect(pages[:]), centred[:], factor[:], ALU.mult)
+
+        for h, queue in enumerate((nc.sync, nc.scalar)):
+            cols = slice(h * U // 2, (h + 1) * U // 2)
+            result = sb.tile([P, U // 2], F32, name="result%d" % h)
+            nc.vector.tensor_tensor(result[:], placed[:, cols], old_sb[:, cols], ALU.add)
+            queue.dma_start(out=out[:, cols], in_=result[:])

@@ -26,8 +26,8 @@ LIST = 16
 VALS_ROW0 = 4
 
 
-def load_scales(queue, plane, scales, row0):
-    for r in range(4):
+def load_scales(queues, plane, scales, row0):
+    for r, queue in enumerate(queues):
         queue.dma_start(out=plane[row0 + r : P : 32, :].bitcast(I32), in_=scales[0, r:16:4, :].bitcast(I32))
 
 
@@ -41,43 +41,56 @@ def tile_attend_bpagepower_kernel(tc, query, keys_words, keys_scales, ptab, gout
         pages = sb.tile([P, G // LIST], U16)
         k_plane = sb.tile([P, T], U8, align_bytes=64, tag="k_plane")
         v_plane = sb.tile([P, T], U8, align_bytes=64)
-        k_store = sb.tile([P, T], U32, align_bytes=64, tag="k_store")
-        v_store = sb.tile([P, T], U32, align_bytes=64, tag="v_store")
-        q_raw = sb.tile([P, PACK, Q], F32)
+        k_store = sb.tile([P, T], U32, align_bytes=64)
+        q_raw = sb.tile([P, PACK, Q], F32, align_bytes=64, tag="v_store")
         g_raw = sb.tile([P, PACK, Q], F32)
         ptab_sb = sb.tile([P, U], F32)
-        old_sb = sb.tile([P, U], F32)
         placed = sb.tile([P, U], F32)
 
         nc.vector.memset(k_plane[:].bitcast(I32), 0)
-        nc.vector.memset(placed[:], 0.0)
         nc.vector.memset(v_plane[:].bitcast(I32), 0)
+        nc.vector.memset(placed[:], 0.0)
 
-        load_scales(nc.sync, k_plane, keys_scales, 0)
+        load_scales((nc.sync, nc.scalar, nc.sync, nc.scalar), k_plane, keys_scales, 0)
+        load_scales((nc.scalar,) * 4, v_plane, vals_scales, VALS_ROW0)
         nc.sync.dma_start(slots[:], offs)
-        nc.sync.dma_start(pages[:], offs2)
         nc.sync.dma_start(out=q_raw[:], in_=query.rearrange("(p j) q -> p j q", j=PACK))
-        nc.sync.dma_start(out=k_store[:].bitcast(I32), in_=keys_words[0].rearrange("p n t -> p (n t)").bitcast(I32))
-        load_scales(nc.scalar, v_plane, vals_scales, VALS_ROW0)
         nc.sync.dma_start(out=g_raw[:], in_=gout.rearrange("(p j) q -> p j q", j=PACK))
+        nc.sync.dma_start(pages[:], offs2)
         nc.sync.dma_start(out=ptab_sb[:], in_=ptab)
-        nc.sync.dma_start(out=v_store[:].bitcast(I32), in_=vals_words[0].rearrange("p n t -> p (n t)").bitcast(I32))
-        nc.sync.dma_start(out=old_sb[:], in_=old)
+        nc.sync.dma_start(out=k_store[:].bitcast(I32), in_=keys_words[0].rearrange("p n t -> p (n t)").bitcast(I32))
 
-        def quantise(raw, name, tag):
+        def round_and_group(raw, name):
             grouped = sb.tile([P, Q, PACK], BF16, align_bytes=64, name=name + "_bf16")
-            codes = sb.tile([P, Q], U32, align_bytes=64, name=name + "_codes", tag=tag)
+            nc.vector.tensor_copy(out=grouped[:], in_=raw[:].rearrange("p j q -> p q j"))
+            return grouped
+
+        def quantise(grouped, name):
+            codes = sb.tile([P, Q], U32, align_bytes=64, name=name + "_codes")
             scales = sb.tile([P, Q], U8, align_bytes=64, name=name + "_scales")
-            nc.scalar.copy(out=grouped[:], in_=raw[:].rearrange("p j q -> p q j"))
             nc.vector.quantize_mx(out=codes[:].bitcast(FP8X4), scales=scales[:], in_=grouped[:].rearrange("p q j -> p (q j)"))
             return codes, scales
+
+        q_bf16 = round_and_group(q_raw, "q")
+        g_bf16 = round_and_group(g_raw, "g")
+        q_codes, q_scales = quantise(q_bf16, "q")
+        g_codes, g_scales = quantise(g_bf16, "g")
+
+        v_store = sb.tile([P, T], U32, align_bytes=64, tag="v_store")
+        nc.sync.dma_start(out=v_store[:].bitcast(I32), in_=vals_words[0].rearrange("p n t -> p (n t)").bitcast(I32))
+
+        log_power = sb.tile([P, G], F32)
+        powers = sb.tile([P, 2, G], F32)
+        nc.vector.tensor_copy(log_power[:], ptab_sb[:].indirect(pages[:]))
+        nc.scalar.activation(powers[:, 0, :], log_power[:], ACT.Exp)
+        nc.scalar.activation(powers[:, 1, :], powers[:, 0, :], ACT.Copy, bias=-1.0)
 
         k_scales = sb.tile([P, I], U8, align_bytes=64)
         v_scales = sb.tile([P, I], U8, align_bytes=64)
         nc.vector.tensor_copy(k_scales[:], k_plane[:].indirect(slots[:]))
-        q_codes, q_scales = quantise(q_raw, "q", "k_plane")
-
         nc.vector.tensor_copy(v_scales[:], v_plane[:].indirect(slots[:]))
+        old_sb = sb.tile([P, U], F32, align_bytes=64, tag="k_plane")
+        nc.sync.dma_start(out=old_sb[:], in_=old)
 
         def product(store, scales, row0, codes_q, scales_q, h, name):
             cols = slice(h * HALF, (h + 1) * HALF)
@@ -101,13 +114,6 @@ def tile_attend_bpagepower_kernel(tc, query, keys_words, keys_scales, ptab, gout
             x = sb.tile([P, HALF], F32, name="x1_%d" % h)
             nc.scalar.activation(x[:], bank[:], ACT.Exp)
             x1.append(x)
-        g_codes, g_scales = quantise(g_raw, "g", "k_store")
-        log_power = sb.tile([P, G], F32)
-        powers = sb.tile([P, 2, G], F32)
-        nc.vector.tensor_copy(log_power[:], ptab_sb[:].indirect(pages[:]))
-        nc.scalar.activation(powers[:, 0, :], log_power[:], ACT.Exp)
-        nc.scalar.activation(powers[:, 1, :], powers[:, 0, :], ACT.Copy, bias=-1.0)
-
         s = sb.tile([P, G], F32)
         for h in range(HALVES):
             nc.vector.tensor_reduce(

@@ -39,31 +39,22 @@ def tile_attend_bpagepower_kernel(tc, query, keys_words, keys_scales, ptab, gout
 
         slots = sb.tile([P, I // LIST], U16)
         pages = sb.tile([P, G // LIST], U16)
-        k_plane = sb.tile([P, T], U8, align_bytes=64, tag="k_plane")
+        k_plane = sb.tile([P, T], U8, align_bytes=64, tag="then_old")
         v_plane = sb.tile([P, T], U8, align_bytes=64)
-        k_store = sb.tile([P, T], U32, align_bytes=64)
-        q_raw = sb.tile([P, PACK, Q], F32, align_bytes=64, tag="v_store")
-        g_raw = sb.tile([P, PACK, Q], F32)
-        ptab_sb = sb.tile([P, U], F32)
+        q_raw = sb.tile([P, PACK, Q], F32, align_bytes=64, tag="then_keys")
+        g_raw = sb.tile([P, PACK, Q], F32, align_bytes=64, tag="then_ptab")
         placed = sb.tile([P, U], F32)
 
         nc.vector.memset(k_plane[:].bitcast(I32), 0)
         nc.vector.memset(v_plane[:].bitcast(I32), 0)
         nc.vector.memset(placed[:], 0.0)
 
-        load_scales((nc.sync, nc.scalar, nc.sync, nc.scalar), k_plane, keys_scales, 0)
-        load_scales((nc.scalar,) * 4, v_plane, vals_scales, VALS_ROW0)
+        load_scales((nc.scalar,) * 4, k_plane, keys_scales, 0)
+        load_scales((nc.sync,) * 4, v_plane, vals_scales, VALS_ROW0)
         nc.sync.dma_start(slots[:], offs)
+        nc.sync.dma_start(pages[:], offs2)
         nc.sync.dma_start(out=q_raw[:], in_=query.rearrange("(p j) q -> p j q", j=PACK))
         nc.sync.dma_start(out=g_raw[:], in_=gout.rearrange("(p j) q -> p j q", j=PACK))
-        nc.sync.dma_start(pages[:], offs2)
-        nc.sync.dma_start(out=ptab_sb[:], in_=ptab)
-        nc.sync.dma_start(out=k_store[:].bitcast(I32), in_=keys_words[0].rearrange("p n t -> p (n t)").bitcast(I32))
-
-        def round_and_group(raw, name):
-            grouped = sb.tile([P, Q, PACK], BF16, align_bytes=64, name=name + "_bf16")
-            nc.vector.tensor_copy(out=grouped[:], in_=raw[:].rearrange("p j q -> p q j"))
-            return grouped
 
         def quantise(grouped, name):
             codes = sb.tile([P, Q], U32, align_bytes=64, name=name + "_codes")
@@ -71,25 +62,25 @@ def tile_attend_bpagepower_kernel(tc, query, keys_words, keys_scales, ptab, gout
             nc.vector.quantize_mx(out=codes[:].bitcast(FP8X4), scales=scales[:], in_=grouped[:].rearrange("p q j -> p (q j)"))
             return codes, scales
 
-        q_bf16 = round_and_group(q_raw, "q")
-        g_bf16 = round_and_group(g_raw, "g")
+        q_bf16 = sb.tile([P, Q, PACK], BF16, align_bytes=64, tag="then_vals")
+        g_bf16 = sb.tile([P, Q, PACK], BF16, align_bytes=64)
+        nc.vector.tensor_copy(out=q_bf16[:], in_=q_raw[:].rearrange("p j q -> p q j"))
+        nc.vector.tensor_copy(out=g_bf16[:], in_=g_raw[:].rearrange("p j q -> p q j"))
         q_codes, q_scales = quantise(q_bf16, "q")
         g_codes, g_scales = quantise(g_bf16, "g")
 
-        v_store = sb.tile([P, T], U32, align_bytes=64, tag="v_store")
+        k_store = sb.tile([P, T], U32, align_bytes=64, tag="then_keys")
+        ptab_sb = sb.tile([P, U], F32, align_bytes=64, tag="then_ptab")
+        v_store = sb.tile([P, T], U32, align_bytes=64, tag="then_vals")
+        nc.sync.dma_start(out=k_store[:].bitcast(I32), in_=keys_words[0].rearrange("p n t -> p (n t)").bitcast(I32))
+        nc.sync.dma_start(out=ptab_sb[:], in_=ptab)
         nc.sync.dma_start(out=v_store[:].bitcast(I32), in_=vals_words[0].rearrange("p n t -> p (n t)").bitcast(I32))
-
-        log_power = sb.tile([P, G], F32)
-        powers = sb.tile([P, 2, G], F32)
-        nc.vector.tensor_copy(log_power[:], ptab_sb[:].indirect(pages[:]))
-        nc.scalar.activation(powers[:, 0, :], log_power[:], ACT.Exp)
-        nc.scalar.activation(powers[:, 1, :], powers[:, 0, :], ACT.Copy, bias=-1.0)
 
         k_scales = sb.tile([P, I], U8, align_bytes=64)
         v_scales = sb.tile([P, I], U8, align_bytes=64)
         nc.vector.tensor_copy(k_scales[:], k_plane[:].indirect(slots[:]))
         nc.vector.tensor_copy(v_scales[:], v_plane[:].indirect(slots[:]))
-        old_sb = sb.tile([P, U], F32, align_bytes=64, tag="k_plane")
+        old_sb = sb.tile([P, U], F32, align_bytes=64, tag="then_old")
         nc.sync.dma_start(out=old_sb[:], in_=old)
 
         def product(store, scales, row0, codes_q, scales_q, h, name):
@@ -114,6 +105,12 @@ def tile_attend_bpagepower_kernel(tc, query, keys_words, keys_scales, ptab, gout
             x = sb.tile([P, HALF], F32, name="x1_%d" % h)
             nc.scalar.activation(x[:], bank[:], ACT.Exp)
             x1.append(x)
+        log_power = sb.tile([P, G], F32)
+        powers = sb.tile([P, 2, G], F32)
+        nc.vector.tensor_copy(log_power[:], ptab_sb[:].indirect(pages[:]))
+        nc.scalar.activation(powers[:, 0, :], log_power[:], ACT.Exp)
+        nc.scalar.activation(powers[:, 1, :], powers[:, 0, :], ACT.Copy, bias=-1.0)
+
         s = sb.tile([P, G], F32)
         for h in range(HALVES):
             nc.vector.tensor_reduce(
@@ -124,9 +121,9 @@ def tile_attend_bpagepower_kernel(tc, query, keys_words, keys_scales, ptab, gout
 
         c_banks = [product(v_store, v_scales, VALS_ROW0, g_codes, g_scales, h, "v") for h in range(HALVES)]
 
-        expo = sb.tile([P, 2, G], F32, align_bytes=64, tag="v_store")
-        neg_top = sb.tile([P, 1], F32)
-        nc.vector.tensor_tensor(expo[:], powers[:], log_s[:].unsqueeze(1).to_broadcast([P, 2, G]), ALU.mult)
+        expo = sb.tile([P, 2, G], F32)
+        neg_top = sb.tile([P, 1], F32, align_bytes=64, tag="then_vals")
+        nc.gpsimd.tensor_tensor(expo[:], powers[:], log_s[:].unsqueeze(1).to_broadcast([P, 2, G]), ALU.mult)
         nc.vector.tensor_reduce(out=neg_top[:], in_=expo[:, 0, :], axis=AXIS.X, op=ALU.max, negate=True)
 
         part = sb.tile([P, G], F32)
@@ -138,15 +135,23 @@ def tile_attend_bpagepower_kernel(tc, query, keys_words, keys_scales, ptab, gout
         nc.scalar.activation(part[:], expo[:, 0, :], ACT.Exp, bias=neg_top[:], accum_out=z[:])
         nc.scalar.activation(part_over_s[:], expo[:, 1, :], ACT.Exp, bias=neg_top[:])
 
-        weighted = sb.tile([P, I], F32)
-        nc.vector.tensor_tensor(weighted[:, 0:HALF], c_banks[0][:], x1[0][:], ALU.mult)
-        nc.vector.tensor_tensor(weighted[:, HALF:I], c_banks[1][:], x1[1][:], ALU.mult)
-        nc.vector.reciprocal(inv_z[:], z[:])
-        nc.scalar.activation(share[:], part[:], ACT.Copy, scale=inv_z[:])
-        nc.scalar.activation(factor[:], expo[:, 0, :], ACT.Copy, scale=inv_z[:])
-
         page_sum = sb.tile([P, G], F32)
-        nc.vector.tensor_reduce(out=page_sum[:], in_=weighted[:].rearrange("p (g i) -> p g i", i=PAGE), axis=AXIS.X, op=ALU.add)
+        for h in range(HALVES):
+            pieces = []
+            for c in range(2):
+                cols = slice(c * HALF // 2, (c + 1) * HALF // 2)
+                weighted = sb.tile([P, HALF // 2], F32, name="weighted%d%d" % (h, c))
+                nc.vector.tensor_tensor(weighted[:], c_banks[h][:, cols], x1[h][:, cols], ALU.mult)
+                pieces.append(weighted)
+            if h == HALVES - 1:
+                nc.vector.reciprocal(inv_z[:], z[:])
+                nc.scalar.activation(share[:], part[:], ACT.Copy, scale=inv_z[:])
+                nc.scalar.activation(factor[:], expo[:, 0, :], ACT.Copy, scale=inv_z[:])
+            for c in range(2):
+                g0 = h * PAGES + c * PAGES // 2
+                nc.vector.tensor_reduce(
+                    out=page_sum[:, g0 : g0 + PAGES // 2], in_=pieces[c][:].rearrange("p (g i) -> p g i", i=PAGE), axis=AXIS.X, op=ALU.add
+                )
 
         term = sb.tile([P, G], F32)
         term_sum = sb.tile([P, 1], F32)

from contextlib import ExitStack

import concourse.mybir as mybir

D, E, T, I, G, U, Q = 512, 512, 4096, 1024, 64, 512, 128
FLOPS = 2 * Q * I * (D + E)

F32 = mybir.dt.float32
BF16 = mybir.dt.bfloat16
I32 = mybir.dt.int32
U32 = mybir.dt.uint32
U16 = mybir.dt.uint16
U8 = mybir.dt.uint8
FP8X4 = mybir.dt.float8_e4m3fn_x4
ALU = mybir.AluOpType
ACT = mybir.ActivationFunctionType
AXIS = mybir.AxisListType

P = 128
PACK = 4
HALF = 512
HALVES = I // HALF
PAGE = I // G
PAGES = HALF // PAGE
LIST = 16
VALS_ROW0 = 4


def load_scales(queues, plane, scales, row0):
    for r, queue in enumerate(queues):
        queue.dma_start(out=plane[row0 + r : P : 32, :].bitcast(I32), in_=scales[0, r:16:4, :].bitcast(I32))


def tile_attend_bpagepower_kernel(tc, query, keys_words, keys_scales, ptab, gout, vals_words, vals_scales, old, offs, offs2, out):
    nc = tc.nc
    with ExitStack() as ctx:
        sb = ctx.enter_context(tc.tile_pool(name="sb", bufs=1))
        ps = ctx.enter_context(tc.psum_pool(name="ps", bufs=1))

        slots = sb.tile([P, I // LIST], U16)
        pages = sb.tile([P, G // LIST], U16)
        k_plane = sb.tile([P, T], U8, align_bytes=64, tag="then_old")
        v_plane = sb.tile([P, T], U8, align_bytes=64)
        q_raw = sb.tile([P, PACK, Q], F32, align_bytes=64, tag="then_keys")
        g_raw = sb.tile([P, PACK, Q], F32, align_bytes=64, tag="then_ptab")
        placed = sb.tile([P, U], F32)

        nc.vector.memset(k_plane[:].bitcast(I32), 0)
        nc.vector.memset(v_plane[:].bitcast(I32), 0)
        nc.vector.memset(placed[:], 0.0)

        load_scales((nc.scalar,) * 4, k_plane, keys_scales, 0)
        load_scales((nc.sync,) * 4, v_plane, vals_scales, VALS_ROW0)
        nc.sync.dma_start(slots[:], offs)
        nc.sync.dma_start(pages[:], offs2)
        nc.sync.dma_start(out=q_raw[:], in_=query.rearrange("(p j) q -> p j q", j=PACK))
        nc.sync.dma_start(out=g_raw[:], in_=gout.rearrange("(p j) q -> p j q", j=PACK))

        def quantise(grouped, name):
            codes = sb.tile([P, Q], U32, align_bytes=64, name=name + "_codes")
            scales = sb.tile([P, Q], U8, align_bytes=64, name=name + "_scales")
            nc.vector.quantize_mx(out=codes[:].bitcast(FP8X4), scales=scales[:], in_=grouped[:].rearrange("p q j -> p (q j)"))
            return codes, scales

        q_bf16 = sb.tile([P, Q, PACK], BF16, align_bytes=64, tag="then_vals")
        g_bf16 = sb.tile([P, Q, PACK], BF16, align_bytes=64)
        nc.vector.tensor_copy(out=q_bf16[:], in_=q_raw[:].rearrange("p j q -> p q j"))
        nc.vector.tensor_copy(out=g_bf16[:], in_=g_raw[:].rearrange("p j q -> p q j"))
        q_codes, q_scales = quantise(q_bf16, "q")
        g_codes, g_scales = quantise(g_bf16, "g")

        k_store = sb.tile([P, T], U32, align_bytes=64, tag="then_keys")
        ptab_sb = sb.tile([P, U], F32, align_bytes=64, tag="then_ptab")
        v_store = sb.tile([P, T], U32, align_bytes=64, tag="then_vals")
        nc.sync.dma_start(out=k_store[:].bitcast(I32), in_=keys_words[0].rearrange("p n t -> p (n t)").bitcast(I32))
        nc.sync.dma_start(out=ptab_sb[:], in_=ptab)
        nc.sync.dma_start(out=v_store[:].bitcast(I32), in_=vals_words[0].rearrange("p n t -> p (n t)").bitcast(I32))

        k_scales = sb.tile([P, I], U8, align_bytes=64)
        v_scales = sb.tile([P, I], U8, align_bytes=64)
        nc.vector.tensor_copy(k_scales[:], k_plane[:].indirect(slots[:]))
        nc.vector.tensor_copy(v_scales[:], v_plane[:].indirect(slots[:]))
        old_sb = sb.tile([P, U], F32, align_bytes=64, tag="then_old")
        nc.sync.dma_start(out=old_sb[:], in_=old)

        def product(store, scales, row0, codes_q, scales_q, h, name):
            cols = slice(h * HALF, (h + 1) * HALF)
            words = sb.tile([P, HALF], U32, align_bytes=64, name="%s_words%d" % (name, h))
            bank = ps.tile([P, HALF], F32, name="%s_bank%d" % (name, h))
            nc.vector.tensor_copy(words[:], store[:].indirect(slots[:, h * HALF // LIST : (h + 1) * HALF // LIST]))
            nc.tensor.matmul_mx(
                out=bank[:],
                lhsT=codes_q[:].bitcast(FP8X4),
                lhsT_scale=scales_q[:],
                rhs=words[:].bitcast(FP8X4),
                rhs_scale=scales[row0:P, cols],
                start=True,
                stop=True,
            )
            return bank

        x1 = []
        for h in range(HALVES):
            bank = product(k_store, k_scales, 0, q_codes, q_scales, h, "k")
            x = sb.tile([P, HALF], F32, name="x1_%d" % h)
            nc.scalar.activation(x[:], bank[:], ACT.Exp)
            x1.append(x)
        log_power = sb.tile([P, G], F32)
        powers = sb.tile([P, 2, G], F32)
        nc.vector.tensor_copy(log_power[:], ptab_sb[:].indirect(pages[:]))
        nc.scalar.activation(powers[:, 0, :], log_power[:], ACT.Exp)
        nc.scalar.activation(powers[:, 1, :], powers[:, 0, :], ACT.Copy, bias=-1.0)

        s = sb.tile([P, G], F32)
        for h in range(HALVES):
            nc.vector.tensor_reduce(
                out=s[:, h * PAGES : (h + 1) * PAGES], in_=x1[h][:].rearrange("p (g i) -> p g i", i=PAGE), axis=AXIS.X, op=ALU.add
            )
        log_s = sb.tile([P, G], F32)
        nc.scalar.activation(log_s[:], s[:], ACT.Ln)

        c_banks = [product(v_store, v_scales, VALS_ROW0, g_codes, g_scales, h, "v") for h in range(HALVES)]

        expo = sb.tile([P, 2, G], F32)
        neg_top = sb.tile([P, 1], F32, align_bytes=64, tag="then_vals")
        nc.gpsimd.tensor_tensor(expo[:], powers[:], log_s[:].unsqueeze(1).to_broadcast([P, 2, G]), ALU.mult)
        nc.vector.tensor_reduce(out=neg_top[:], in_=expo[:, 0, :], axis=AXIS.X, op=ALU.max, negate=True)

        part = sb.tile([P, G], F32)
        part_over_s = sb.tile([P, G], F32)
        z = sb.tile([P, 1], F32)
        inv_z = sb.tile([P, 1], F32)
        share = sb.tile([P, G], F32)
        factor = sb.tile([P, G], F32)
        nc.scalar.activation(part[:], expo[:, 0, :], ACT.Exp, bias=neg_top[:], accum_out=z[:])
        nc.scalar.activation(part_over_s[:], expo[:, 1, :], ACT.Exp, bias=neg_top[:])

        page_sum = sb.tile([P, G], F32)
        for h in range(HALVES):
            pieces = []
            for c in range(2):
                cols = slice(c * HALF // 2, (c + 1) * HALF // 2)
                weighted = sb.tile([P, HALF // 2], F32, name="weighted%d%d" % (h, c))
                nc.vector.tensor_tensor(weighted[:], c_banks[h][:, cols], x1[h][:, cols], ALU.mult)
                pieces.append(weighted)
            if h == HALVES - 1:
                nc.vector.reciprocal(inv_z[:], z[:])
                nc.scalar.activation(share[:], part[:], ACT.Copy, scale=inv_z[:])
                nc.scalar.activation(factor[:], expo[:, 0, :], ACT.Copy, scale=inv_z[:])
            for c in range(2):
                g0 = h * PAGES + c * PAGES // 2
                nc.vector.tensor_reduce(
                    out=page_sum[:, g0 : g0 + PAGES // 2], in_=pieces[c][:].rearrange("p (g i) -> p g i", i=PAGE), axis=AXIS.X, op=ALU.add
                )

        term = sb.tile([P, G], F32)
        term_sum = sb.tile([P, 1], F32)
        centred = sb.tile([P, G], F32)
        nc.vector.scalar_tensor_tensor(term[:], page_sum[:], -8.0, part_over_s[:], ALU.mult, ALU.mult, accum_out=term_sum[:])
        nc.vector.scalar_tensor_tensor(centred[:], share[:], term_sum[:], term[:], ALU.mult, ALU.subtract)
        nc.vector.tensor_tensor(placed[:].indirect(pages[:]), centred[:], factor[:], ALU.mult)

        for h, queue in enumerate((nc.sync, nc.scalar)):
            cols = slice(h * U // 2, (h + 1) * U // 2)
            result = sb.tile([P, U // 2], F32, name="result%d" % h)
            nc.vector.tensor_tensor(result[:], placed[:, cols], old_sb[:, cols], ALU.add)
            queue.dma_start(out=out[:, cols], in_=result[:])
